import numpy as np
import ml_dtypes


def mxq(x, axis, fmt="e4m3"):
    dtype, down = {"e4m3": (ml_dtypes.float8_e4m3fn, 7), "e5m2": (ml_dtypes.float8_e5m2, 14)}[fmt]
    v = np.moveaxis(np.asarray(x, np.float32).astype(ml_dtypes.bfloat16).astype(np.float64), axis, -1)
    blocks = v.reshape(v.shape[:-1] + (-1, 32))
    amax = np.abs(blocks).max(-1, keepdims=True)
    byte = np.maximum(np.where(amax > 0, np.frexp(amax)[1] - 1 + 127, 0) - down, 1)
    scale = np.exp2(byte - 127.0)
    codes = (blocks / scale).astype(np.float32).astype(dtype).astype(np.float64)
    return np.moveaxis((codes * scale).reshape(v.shape), -1, axis)


WIDE = False


def mx_kscale(k):
    if not WIDE:
        return np.ones(k)
    levels = np.array([10, -10, 5, -5, 0])
    if k % 512:
        return np.exp2(np.random.permutation(np.resize(levels, k // 32))).repeat(32)
    a = np.empty((k // 512, 16))
    for p in range(k // 512):
        a[p, :8] = np.random.permutation(np.resize(levels, 8))
        for g in range(8):
            far = levels[np.abs(levels - a[p, g]) >= 10]
            a[p, g + 8] = far[np.random.randint(len(far))]
    return np.exp2(a.ravel()).repeat(32)


def f64(x):
    return np.asarray(x).astype(np.float64)


def striped(idx):
    return np.tile(np.asarray(idx).reshape(-1, 16).T, (8, 1)).astype(np.uint16)


def unstriped(offs):
    return offs[:16].T.reshape(-1).astype(np.int64)


E2M1 = np.array([0.0, 0.5, 1.0, 1.5, 2.0, 3.0, 4.0, 6.0, -0.0, -0.5, -1.0, -1.5, -2.0, -3.0, -4.0, -6.0])


def pack_weight(w, fmt):
    k, n = w.shape
    w = f64(np.asarray(w, np.float32).astype(ml_dtypes.bfloat16)).reshape(k // 32, 32, n)
    amax = np.abs(w).max(1)
    if fmt == "e4m3":
        byte = np.frexp(amax)[1] - 1 + 127 - 7
    else:
        mant, ex = np.frexp(amax / 6.0)
        byte = np.where(mant > 0.5, ex, ex - 1) + 127
    byte = np.clip(np.where(amax > 0, byte, 1), 1, 254)
    scaled = (w * np.exp2(127.0 - byte)[:, None, :]).reshape(k, n).astype(np.float32)
    by_word = np.ascontiguousarray(scaled.reshape(k // 512, 128, 4, n).transpose(0, 1, 3, 2))
    if fmt == "e4m3":
        words = by_word.astype(ml_dtypes.float8_e4m3fn).view(np.uint8)
    else:
        c = by_word.astype(ml_dtypes.float4_e2m1fn).view(np.uint8) & 0xF
        words = (c[..., 0::2] | (c[..., 1::2] << 4)).reshape(k // 512, 128, 2 * n)
    return np.ascontiguousarray(words), np.ascontiguousarray(byte.astype(np.uint8).reshape(k // 512, 16, n))


def unpack_weight(words, scales, fmt):
    g, _, n = scales.shape
    words = np.ascontiguousarray(words).reshape(g, 128, n, -1)
    if fmt == "e4m3":
        vals = words.view(ml_dtypes.float8_e4m3fn).astype(np.float64)
    else:
        nib = np.empty((g, 128, n, 4), np.uint8)
        nib[..., 0::2] = words & 0xF
        nib[..., 1::2] = words >> 4
        vals = E2M1[nib]
    vals = vals * np.repeat(np.exp2(scales.astype(np.float64) - 127.0), 8, axis=1)[..., None]
    return vals.transpose(0, 1, 3, 2).reshape(g * 512, n)


def sigmoid(v):
    return 1.0 / (1.0 + np.exp(-v))


D, E, T, I, Q, G, B = 512, 512, 2048, 512, 128, 64, 8


def setup_inputs():
    n = np.random.standard_normal
    idx = np.random.permutation(T)[:I]
    fd = mx_kscale(D)
    fe = mx_kscale(E)
    keysp = pack_weight(n((D, T)) / fd[:, None], "e2m1")
    valsp = pack_weight(n((E, T)) / fe[:, None], "e2m1")
    return {
        "query": (n((D, Q)) * 0.8 / np.sqrt(D) * fd[:, None]).astype(np.float32),
        "keys_words": keysp[0],
        "keys_scales": keysp[1],
        "steep": (np.random.uniform(2.0, 8.0, (Q, 1))).astype(np.float32),
        "gout": (n((E, Q)) * 1 / np.sqrt(E) * fe[:, None]).astype(np.float32),
        "vals_words": valsp[0],
        "vals_scales": valsp[1],
        "base": (0.5 * n((Q, I))).astype(np.float32),
        "offs": striped(idx),
    }


def reference(query, keys_words, keys_scales, steep, gout, vals_words, vals_scales, base, offs):
    idx = unstriped(offs)
    keysu = unpack_weight(keys_words, keys_scales, "e2m1")
    valsu = unpack_weight(vals_words, vals_scales, "e2m1")
    queryq = mxq(f64(query), 0, "e4m3")
    keysidxg = keysu[:, idx]
    a = queryq.T @ keysidxg
    m1 = a.reshape(Q, G, I // G).mean(axis=2)
    m2 = m1.reshape(Q, B, G // B).mean(axis=2)
    mr = np.repeat(m2, G // B, axis=1)
    g1 = sigmoid((m1 - mr) * f64(steep))
    gr = np.repeat(g1, I // G, axis=1)
    p = np.exp(a) * gr
    z = np.sum(p, axis=1, keepdims=True)
    goutq = mxq(f64(gout), 0, "e4m3")
    valsidxg = valsu[:, idx]
    c0 = goutq.T @ valsidxg
    dz = np.sum(c0 * p / np.square(z) * (-1.0), axis=1, keepdims=True)
    dp = c0 / z + dz
    dgr = dp * np.exp(a)
    dg1 = dgr.reshape(Q, G, I // G).sum(axis=2)
    dmr = dg1 * g1 * (1.0 - g1) * f64(steep) * (-1.0)
    dm2 = dmr.reshape(Q, B, G // B).sum(axis=2)
    e1 = dm2 / 8.0
    r1 = np.repeat(e1, G // B, axis=1)
    dm1 = dg1 * g1 * (1.0 - g1) * f64(steep) + r1
    e2 = dm1 / 8.0
    r2 = np.repeat(e2, I // G, axis=1)
    da = dp * gr * np.exp(a) + r2
    hda = da * 512.0 * 2.0 * 512.0
    he2 = hda.reshape(Q, G, I // G).sum(axis=2)
    hdm1 = he2 / 8.0
    he1 = hdm1.reshape(Q, B, G // B).sum(axis=2)
    hdm2 = he1 / 8.0
    r51 = np.repeat(hdm2, G // B, axis=1)
    hdg1 = hdm1 * f64(steep) * (1.0 - g1) * g1 + r51 * (-1.0) * f64(steep) * (1.0 - g1) * g1
    r52 = np.repeat(hdg1, I // G, axis=1)
    hdp = hda * np.exp(a) * gr + r52 * np.exp(a)
    hdz = np.sum(hdp, axis=1, keepdims=True)
    hz = np.sum(hdp * c0 / np.square(z) * (-1.0), axis=1, keepdims=True) + np.sum(hdz * (-1.0) * c0 * p / np.square(np.square(z)) * (-1.0), axis=1, keepdims=True) * z * 2.0
    hp = hdz * (-1.0) / np.square(z) * c0 + hz
    hgr = hda * np.exp(a) * dp + hp * np.exp(a)
    hg1 = hdm1 * f64(steep) * (1.0 - g1) * dg1 + r51 * (-1.0) * f64(steep) * (1.0 - g1) * dg1 + hgr.reshape(Q, G, I // G).sum(axis=2) - hdm1 * f64(steep) * dg1 * g1 - r51 * (-1.0) * f64(steep) * dg1 * g1
    hmr = hg1 * g1 * (1.0 - g1) * f64(steep) * (-1.0)
    hm2 = hmr.reshape(Q, B, G // B).sum(axis=2)
    e53 = hm2 / 8.0
    r53 = np.repeat(e53, G // B, axis=1)
    hm1 = hg1 * g1 * (1.0 - g1) * f64(steep) + r53
    e54 = hm1 / 8.0
    r54 = np.repeat(e54, I // G, axis=1)
    ha = hda * dp * gr * np.exp(a) + r52 * dp * np.exp(a) + hp * gr * np.exp(a) + r54
    y = ha + f64(base)
    return y

@@ -1,0 +1,295 @@
+import math
+from contextlib import ExitStack
+
+import concourse.mybir as mybir
+
+F32 = mybir.dt.float32
+BF16 = mybir.dt.bfloat16
+I32 = mybir.dt.int32
+U32 = mybir.dt.uint32
+U16 = mybir.dt.uint16
+U8 = mybir.dt.uint8
+FP8X4 = mybir.dt.float8_e4m3fn_x4
+FP4X4 = mybir.dt.float4_e2m1fn_x4
+ACT = mybir.ActivationFunctionType
+ALU = mybir.AluOpType
+AXIS = mybir.AxisListType
+
+P = 128
+PACK = 4
+POOL = 2048
+SLOTS = 512
+RUN = 8
+GROUPS = SLOTS // RUN
+BLOCKS = GROUPS // RUN
+PENALTY = 512.0 * 2.0 * 512.0
+
+FLOPS = 2 * 2 * 512 * P * SLOTS
+
+
+def runs(ap):
+    return ap.rearrange("p (n j) -> p n j", j=RUN)
+
+
+def spread(ap):
+    return ap.unsqueeze(2).to_broadcast([P, ap.shape[1], RUN])
+
+
+def times(ap, n):
+    return ap.unsqueeze(1).to_broadcast([P, n, ap.shape[1]])
+
+
+def tile_attend_gpblockcontrast_kernel(tc, query, keys_words, keys_scales, steep, gout, vals_words, vals_scales, base, offs, out):
+    nc = tc.nc
+    vec, act = nc.vector, nc.scalar
+    G = GROUPS
+
+    with ExitStack() as ctx:
+        sb = ctx.enter_context(tc.tile_pool(name="sb", bufs=1))
+        ps = ctx.enter_context(tc.psum_pool(name="ps", bufs=1))
+
+        def wide(name):
+            return sb.tile([P, SLOTS], F32, name=name)
+
+        def small(name, width, tag=None):
+            if tag is None:
+                return sb.tile([P, width], F32, name=name)
+            return sb.tile([P, width], F32, name=name, tag=tag, align_bytes=64)
+
+        def centre(dst, src, name):
+            n = src.shape[1] // RUN
+            sums = small(name, n)
+            vec.tensor_reduce(out=sums[:], in_=runs(src), axis=AXIS.X, op=ALU.add)
+            return lambda: vec.scalar_tensor_tensor(
+                out=runs(dst), in0=spread(sums[:]), scalar=-1.0 / RUN, in1=runs(src), op0=ALU.mult, op1=ALU.add
+            )
+
+        offsets = sb.tile([P, SLOTS // 16], U16, name="offsets")
+        k_bytes = sb.tile([P, POOL], U8, name="k_bytes")
+        v_bytes = sb.tile([P, POOL], U8, name="v_bytes")
+        k_words = sb.tile([P, POOL], U16, name="k_words")
+        v_words = sb.tile([P, POOL], U16, name="v_words")
+        q_raw = sb.tile([P, PACK, P], F32, name="q_raw", tag="q_then_base")
+        g_raw = sb.tile([P, PACK, P], F32, name="g_raw")
+        s_col = small("s_col", 1)
+
+        nc.gpsimd.memset(k_bytes[:].bitcast(I32), 0)
+        vec.memset(v_bytes[:].bitcast(I32), 0)
+        nc.sync.dma_start(offsets[:], offs)
+        for quad in range(4):
+            nc.sync.dma_start(
+                k_bytes[32 * quad : 32 * quad + 4, :].bitcast(I32), keys_scales[0, 4 * quad : 4 * quad + 4, :].bitcast(I32)
+            )
+        nc.sync.dma_start(k_words[:].bitcast(I32), keys_words[0].bitcast(I32))
+        nc.sync.dma_start(q_raw[:], query.rearrange("(p j) w -> p j w", j=PACK))
+        nc.sync.dma_start(g_raw[:], gout.rearrange("(p j) w -> p j w", j=PACK))
+        nc.sync.dma_start(v_words[:].bitcast(I32), vals_words[0].bitcast(I32))
+        for quad in range(4):
+            nc.sync.dma_start(
+                v_bytes[32 * quad : 32 * quad + 4, :].bitcast(I32), vals_scales[0, 4 * quad : 4 * quad + 4, :].bitcast(I32)
+            )
+        nc.gpsimd.dma_start(s_col[:], steep)
+
+        s_mult = small("s_mult", 5)
+        for col, (factor, plus) in enumerate(((1.0 / 16, 0.0), (-0.5, 0.0), (0.5, 0.0), (0.5, 1.0), (-1.0, 0.0))):
+            nc.gpsimd.tensor_scalar(
+                out=s_mult[:, col : col + 1], in0=s_col[:], scalar1=factor, scalar2=plus, op0=ALU.mult, op1=ALU.add
+            )
+        s_16th, s_neg_half, s_half, s_half_1, s_neg = (s_mult[:, col : col + 1] for col in range(5))
+
+        slopes = sb.tile([P, 4, G], F32, name="slopes")
+        nc.gpsimd.memset(slopes[:, 2, :], 1.0)
+        xs = small("xs", 200)
+        vec.memset(xs[:, 3:197:193], 8.0)
+
+        def quantise(raw, name):
+            woven = sb.tile([P, P, PACK], BF16, name=name + "_woven", tag=name + "_woven", align_bytes=64)
+            codes = sb.tile([P, P], U32, name=name + "_codes", align_bytes=64)
+            scales = sb.tile([P, P], U8, name=name + "_scales", align_bytes=64)
+            act.activation(out=woven[:], in_=raw[:].rearrange("p j w -> p w j"), func=ACT.Copy)
+            return codes, scales, lambda: vec.quantize_mx(
+                out=codes[:].bitcast(FP8X4), scales=scales[:], in_=woven[:].rearrange("p w j -> p (w j)")
+            )
+
+        def gather(window, dtype, name, tag=None, first=0, count=SLOTS):
+            got = sb.tile([P, count], dtype, name=name, tag=tag or name, align_bytes=64)
+            vec.tensor_copy(out=got[:], in_=window[:].indirect(offsets[:, first // 16 : (first + count) // 16]))
+            return got
+
+        q_codes, q_scales, q_quant = quantise(q_raw, "q")
+        g_codes, g_scales, g_quant = quantise(g_raw, "g")
+        base_sb = sb.tile([P, SLOTS], F32, name="base_sb", tag="q_then_base")
+        nc.sync.dma_start(base_sb[:], base)
+
+        kb = gather(k_bytes, U8, "kb")
+        kw = gather(k_words, U16, "kw")
+        q_quant()
+        a_ps = ps.tile([P, SLOTS], F32, name="a_ps")
+        nc.tensor.matmul_mx(
+            out=a_ps[:], lhsT=q_codes[:].bitcast(FP8X4), lhsT_scale=q_scales[:],
+            rhs=kw[:].bitcast(FP4X4), rhs_scale=kb[:], start=True, stop=True,
+        )
+        vw = gather(v_words, U16, "vw", tag="q_woven")
+        g_quant()
+        c_ps = ps.tile([P, SLOTS], F32, name="c_ps")
+
+        def values_half(h, tag):
+            cols = slice(h * SLOTS // 2, (h + 1) * SLOTS // 2)
+            vb = gather(v_bytes, U8, "vb%d" % h, tag=tag, first=cols.start, count=SLOTS // 2)
+            nc.tensor.matmul_mx(
+                out=c_ps[:, cols], lhsT=g_codes[:].bitcast(FP8X4), lhsT_scale=g_scales[:],
+                rhs=vw[:, cols].bitcast(FP4X4), rhs_scale=vb[:], start=True, stop=True,
+            )
+
+        values_half(0, "kb")
+
+        root = wide("root")
+        root_sum = small("root_sum", 1, tag="root_sum")
+        act.activation(out=root[:], in_=a_ps[:], func=ACT.Exp, scale=0.25, accum_out=root_sum[:])
+        root_inv = small("root_inv", 1)
+        vec.reciprocal(out=root_inv[:], in_=root_sum[:])
+        half = wide("half")
+        act.activation(out=half[:], in_=root[:], func=ACT.Square, scale=root_inv[:])
+        e = wide("e")
+        act.activation(out=e[:], in_=half[:], func=ACT.Square)
+
+        a_sum = small("a_sum", G, tag="a_sum")
+        vec.tensor_reduce(out=a_sum[:], in_=runs(a_ps[:]), axis=AXIS.X, op=ALU.add)
+        contrast = small("contrast", G)
+        centre(contrast[:], a_sum[:], "a_blocks")()
+        values_half(1, "a_sum")
+
+        th = small("th", G)
+        act.activation(out=th[:], in_=contrast[:], func=ACT.Tanh, scale=s_16th)
+        act.activation(out=slopes[:, 1, :], in_=th[:], func=ACT.Identity, scale=s_neg_half, bias=s_half)
+        act.activation(out=slopes[:, 0, :], in_=th[:], func=ACT.Identity, scale=s_neg_half, bias=s_half_1)
+        act.activation(out=slopes[:, 3, :], in_=th[:], func=ACT.Copy, scale=s_neg)
+
+        left, right = slice(0, SLOTS // 2), slice(SLOTS // 2, SLOTS)
+        p = wide("p")
+        z = small("z", 1)
+        vec.scalar_tensor_tensor(
+            out=runs(p[:]), in0=spread(th[:]), scalar=1.0, in1=runs(e[:]), op0=ALU.add, op1=ALU.mult, accum_out=z[:]
+        )
+        mass = small("mass", G)
+        vec.tensor_reduce(out=mass[:, 0 : G // 2], in_=runs(p[:, left]), axis=AXIS.X, op=ALU.add)
+        z_inv = small("z_inv", 1)
+        vec.reciprocal(out=z_inv[:], in_=z[:])
+        vec.tensor_reduce(out=mass[:, G // 2 : G], in_=runs(p[:, right]), axis=AXIS.X, op=ALU.add)
+        z_mult = small("z_mult", 6)
+        z_16th, z_half, root_k, two_k, quarter_k, neg_four = (z_mult[:, col : col + 1] for col in range(6))
+        act.activation(out=z_16th, in_=z[:], func=ACT.Copy, scale=1.0 / 16)
+        act.activation(out=z_half, in_=z[:], func=ACT.Copy, scale=0.5)
+        act.activation(out=root_k, in_=z_inv[:], func=ACT.Copy, scale=math.sqrt(PENALTY))
+        act.activation(out=two_k, in_=z_inv[:], func=ACT.Copy, scale=2 * PENALTY)
+        act.activation(out=quarter_k, in_=z_inv[:], func=ACT.Copy, scale=PENALTY / 4)
+        act.activation(out=neg_four, in_=z_inv[:], func=ACT.Copy, scale=-4.0)
+        spare = wide("spare")
+        c_mean = small("c_mean", 1)
+        vec.scalar_tensor_tensor(
+            out=spare[:], in0=c_ps[:], scalar=z_inv[:], in1=p[:], op0=ALU.mult, op1=ALU.mult, accum_out=c_mean[:]
+        )
+        pis = sb.tile([P, 2, G], F32, name="pis")
+        vec.tensor_tensor(out=pis[:], in0=slopes[:, 1:3, :], in1=times(mass[:], 2), op=ALU.mult)
+        y = wide("y")
+        vec.scalar_tensor_tensor(
+            out=y[:], in0=c_ps[:], scalar=c_mean[:], in1=p[:], op0=ALU.subtract, op1=ALU.mult
+        )
+        v_side = small("v_side", 132)
+        centre_pis = centre(v_side[:, 4:132], pis[:].rearrange("p t g -> p (t g)"), "pi_blocks")
+        w_side = small("w_side", 129)
+        y2 = wide("y2")
+        act.activation(out=y2[:], in_=y[:], func=ACT.Square, scale=z_inv[:], accum_out=w_side[:, 128:129])
+
+        y_sum = small("y_sum", G)
+        vec.tensor_reduce(out=y_sum[:], in_=runs(y[:]), axis=AXIS.X, op=ALU.add)
+        centre_pis()
+        vec.scalar_tensor_tensor(
+            out=xs[:, 4:196].rearrange("p (t g) -> p t g", t=3), in0=slopes[:, 0:3, :], scalar=z_inv[:],
+            in1=times(y_sum[:], 3), op0=ALU.mult, op1=ALU.mult,
+        )
+        vec.scalar_tensor_tensor(
+            out=spare[:], in0=p[:], scalar=z_inv[:], in1=y[:], op0=ALU.mult, op1=ALU.mult, accum_out=v_side[:, 3:4]
+        )
+        x_f = xs[:, 68:132]
+        centre_xs = centre(w_side[:, 0:128], xs[:, 4:132], "x_blocks")
+        v_neg = small("v_neg", 1)
+        spare_v = small("spare_v", 129)
+        vec.scalar_tensor_tensor(
+            out=spare_v[:], in0=xs[:, 3:132], scalar=-1.0 / 16, in1=v_side[:, 3:132],
+            op0=ALU.mult, op1=ALU.mult, accum_out=v_neg[:],
+        )
+        centre_xs()
+        y2_sum = small("y2_sum", G)
+        vec.tensor_reduce(out=y2_sum[:, 0 : G // 2], in_=runs(y2[:, left]), axis=AXIS.X, op=ALU.add)
+        h_f = sb.tile([P, 2, G], F32, name="h_f")
+        vec.scalar_tensor_tensor(
+            out=h_f[:], in0=slopes[:, 1:4:2, :], scalar=z_16th, in1=times(w_side[:, 0:64], 2),
+            op0=ALU.mult, op1=ALU.mult,
+        )
+        w_neg = small("w_neg", 1)
+        spare_w = small("spare_w", 129)
+        vec.scalar_tensor_tensor(
+            out=spare_w[:], in0=w_side[:], scalar=-1.0 / 16, in1=xs[:, 68:197],
+            op0=ALU.mult, op1=ALU.mult, accum_out=w_neg[:],
+        )
+        w_neg_p = small("w_neg_p", 1)
+        act.activation(out=w_neg_p[:], in_=w_neg[:], func=ACT.Copy, scale=two_k)
+        coefs = sb.tile([P, 2, G], F32, name="coefs")
+        vec.scalar_tensor_tensor(
+            out=coefs[:], in0=times(w_side[:, 64:128], 2), scalar=z_16th, in1=h_f[:], op0=ALU.mult, op1=ALU.add
+        )
+        vec.tensor_reduce(out=y2_sum[:, G // 2 : G], in_=runs(y2[:, right]), axis=AXIS.X, op=ALU.add)
+        moved = wide("moved")
+        vec.scalar_tensor_tensor(
+            out=runs(moved[:]), in0=spread(coefs[:, 0, :]), scalar=v_neg[:], in1=runs(y[:]), op0=ALU.add, op1=ALU.add
+        )
+        move2 = small("move2", G)
+        act.activation(out=move2[:], in_=coefs[:, 0, :], func=ACT.Square, bias=v_neg[:])
+        square = wide("square")
+        for cols in (left, right):
+            act.activation(out=square[:, cols], in_=moved[:, cols], func=ACT.Square, scale=root_k)
+        n0 = small("n0", G)
+        vec.scalar_tensor_tensor(
+            out=n0[:], in0=y2_sum[:], scalar=z_half, in1=slopes[:, 1, :], op0=ALU.mult, op1=ALU.mult
+        )
+        terms = sb.tile([P, 2, G], F32, name="terms")
+        vec.scalar_tensor_tensor(
+            out=terms[:, 0, :], in0=coefs[:, 1, :], scalar=v_neg[:], in1=x_f, op0=ALU.add, op1=ALU.mult
+        )
+        m_part = small("m_part", G)
+        vec.scalar_tensor_tensor(
+            out=terms[:, 1, :], in0=pis[:, 0, :], scalar=w_neg[:], in1=n0[:], op0=ALU.mult, op1=ALU.add
+        )
+        vec.scalar_tensor_tensor(
+            out=m_part[:], in0=move2[:], scalar=neg_four, in1=terms[:, 0, :], op0=ALU.mult, op1=ALU.add
+        )
+        t2 = wide("t2")
+
+        def add_p(cols):
+            vec.scalar_tensor_tensor(
+                out=t2[:, cols], in0=p[:, cols], scalar=w_neg_p[:], in1=base_sb[:, cols], op0=ALU.mult, op1=ALU.add
+            )
+
+        add_p(left)
+        m_blocks = small("m_blocks", BLOCKS)
+        vec.tensor_reduce(
+            out=m_blocks[:], in_=terms[:].rearrange("p t (b j) -> p b t j", j=RUN), axis=AXIS.XY, op=ALU.add
+        )
+        m_sum = small("m_sum", G)
+        vec.tensor_tensor(out=m_sum[:], in0=m_part[:], in1=terms[:, 1, :], op=ALU.add)
+        add_p(right)
+        shift = small("shift", G)
+        vec.scalar_tensor_tensor(
+            out=runs(shift[:]), in0=spread(m_blocks[:]), scalar=-1.0 / RUN, in1=runs(m_sum[:]), op0=ALU.mult, op1=ALU.add
+        )
+        t3 = wide("t3")
+        result = wide("result")
+        for h, cols in enumerate((left, right)):
+            vec.scalar_tensor_tensor(
+                out=runs(t3[:, cols]), in0=spread(shift[:, h * G // 2 : (h + 1) * G // 2]), scalar=quarter_k,
+                in1=runs(t2[:, cols]), op0=ALU.mult, op1=ALU.add,
+            )
+        for cols, queue in ((left, nc.sync), (right, nc.scalar)):
+            vec.tensor_tensor(out=result[:, cols], in0=t3[:, cols], in1=square[:, cols], op=ALU.add)
+            queue.dma_start(out[:, cols], result[:, cols])

@@ -1,4 +1,3 @@
-import math
 from contextlib import ExitStack
 
 import concourse.mybir as mybir
@@ -73,9 +72,10 @@ def tile_attend_gpblockcontrast_kernel(tc, query, keys_words, keys_scales, steep
         g_raw = sb.tile([P, PACK, P], F32, name="g_raw")
         s_col = small("s_col", 1)
 
-        nc.gpsimd.memset(k_bytes[:].bitcast(I32), 0)
-        vec.memset(v_bytes[:].bitcast(I32), 0)
+        vec.memset(k_bytes[:].bitcast(I32), 0)
+        nc.gpsimd.memset(v_bytes[:].bitcast(I32), 0)
         nc.sync.dma_start(offsets[:], offs)
+        nc.sync.dma_start(s_col[:], steep)
         for quad in range(4):
             nc.sync.dma_start(
                 k_bytes[32 * quad : 32 * quad + 4, :].bitcast(I32), keys_scales[0, 4 * quad : 4 * quad + 4, :].bitcast(I32)
@@ -88,19 +88,19 @@ def tile_attend_gpblockcontrast_kernel(tc, query, keys_words, keys_scales, steep
             nc.sync.dma_start(
                 v_bytes[32 * quad : 32 * quad + 4, :].bitcast(I32), vals_scales[0, 4 * quad : 4 * quad + 4, :].bitcast(I32)
             )
-        nc.gpsimd.dma_start(s_col[:], steep)
 
-        s_mult = small("s_mult", 5)
-        for col, (factor, plus) in enumerate(((1.0 / 16, 0.0), (-0.5, 0.0), (0.5, 0.0), (0.5, 1.0), (-1.0, 0.0))):
-            nc.gpsimd.tensor_scalar(
-                out=s_mult[:, col : col + 1], in0=s_col[:], scalar1=factor, scalar2=plus, op0=ALU.mult, op1=ALU.add
-            )
-        s_16th, s_neg_half, s_half, s_half_1, s_neg = (s_mult[:, col : col + 1] for col in range(5))
+        factors = small("factors", 9)
+        for col, value in enumerate((1.0 / 16, 0.5, -0.5, -1.0, 1.0 / 16, 0.5, 2 * PENALTY, PENALTY / 4, -4.0)):
+            vec.memset(factors[:, col : col + 1], value)
 
+        s_mult = small("s_mult", 4)
+        vec.tensor_scalar(out=s_mult[:], in0=factors[:, 0:4], scalar1=s_col[:], scalar2=None, op0=ALU.mult)
+        s_16th, s_half, s_neg_half, s_neg = (s_mult[:, col : col + 1] for col in range(4))
         slopes = sb.tile([P, 4, G], F32, name="slopes")
-        nc.gpsimd.memset(slopes[:, 2, :], 1.0)
+        vec.memset(slopes[:, 2, :], 1.0)
         xs = small("xs", 200)
-        vec.memset(xs[:, 3:197:193], 8.0)
+        vec.memset(xs[:, 2:4], 8.0)
+        vec.memset(xs[:, 196:197], 8.0)
 
         def quantise(raw, name):
             woven = sb.tile([P, P, PACK], BF16, name=name + "_woven", tag=name + "_woven", align_bytes=64)
@@ -162,8 +162,8 @@ def tile_attend_gpblockcontrast_kernel(tc, query, keys_words, keys_scales, steep
         th = small("th", G)
         act.activation(out=th[:], in_=contrast[:], func=ACT.Tanh, scale=s_16th)
         act.activation(out=slopes[:, 1, :], in_=th[:], func=ACT.Identity, scale=s_neg_half, bias=s_half)
-        act.activation(out=slopes[:, 0, :], in_=th[:], func=ACT.Identity, scale=s_neg_half, bias=s_half_1)
         act.activation(out=slopes[:, 3, :], in_=th[:], func=ACT.Copy, scale=s_neg)
+        act.activation(out=slopes[:, 0, :], in_=slopes[:, 1, :], func=ACT.Copy, bias=1.0)
 
         left, right = slice(0, SLOTS // 2), slice(SLOTS // 2, SLOTS)
         p = wide("p")
@@ -176,14 +176,10 @@ def tile_attend_gpblockcontrast_kernel(tc, query, keys_words, keys_scales, steep
         z_inv = small("z_inv", 1)
         vec.reciprocal(out=z_inv[:], in_=z[:])
         vec.tensor_reduce(out=mass[:, G // 2 : G], in_=runs(p[:, right]), axis=AXIS.X, op=ALU.add)
-        z_mult = small("z_mult", 6)
-        z_16th, z_half, root_k, two_k, quarter_k, neg_four = (z_mult[:, col : col + 1] for col in range(6))
-        act.activation(out=z_16th, in_=z[:], func=ACT.Copy, scale=1.0 / 16)
-        act.activation(out=z_half, in_=z[:], func=ACT.Copy, scale=0.5)
-        act.activation(out=root_k, in_=z_inv[:], func=ACT.Copy, scale=math.sqrt(PENALTY))
-        act.activation(out=two_k, in_=z_inv[:], func=ACT.Copy, scale=2 * PENALTY)
-        act.activation(out=quarter_k, in_=z_inv[:], func=ACT.Copy, scale=PENALTY / 4)
-        act.activation(out=neg_four, in_=z_inv[:], func=ACT.Copy, scale=-4.0)
+        z_mult = small("z_mult", 5)
+        act.activation(out=z_mult[:, 0:2], in_=factors[:, 4:6], func=ACT.Copy, scale=z[:])
+        act.activation(out=z_mult[:, 2:5], in_=factors[:, 6:9], func=ACT.Copy, scale=z_inv[:])
+        z_16th, z_half, two_k, quarter_k, neg_four = (z_mult[:, col : col + 1] for col in range(5))
         spare = wide("spare")
         c_mean = small("c_mean", 1)
         vec.scalar_tensor_tensor(
@@ -203,29 +199,32 @@ def tile_attend_gpblockcontrast_kernel(tc, query, keys_words, keys_scales, steep
 
         y_sum = small("y_sum", G)
         vec.tensor_reduce(out=y_sum[:], in_=runs(y[:]), axis=AXIS.X, op=ALU.add)
-        centre_pis()
         vec.scalar_tensor_tensor(
             out=xs[:, 4:196].rearrange("p (t g) -> p t g", t=3), in0=slopes[:, 0:3, :], scalar=z_inv[:],
             in1=times(y_sum[:], 3), op0=ALU.mult, op1=ALU.mult,
         )
-        vec.scalar_tensor_tensor(
-            out=spare[:], in0=p[:], scalar=z_inv[:], in1=y[:], op0=ALU.mult, op1=ALU.mult, accum_out=v_side[:, 3:4]
-        )
         x_f = xs[:, 68:132]
-        centre_xs = centre(w_side[:, 0:128], xs[:, 4:132], "x_blocks")
-        v_neg = small("v_neg", 1)
-        spare_v = small("spare_v", 129)
-        vec.scalar_tensor_tensor(
-            out=spare_v[:], in0=xs[:, 3:132], scalar=-1.0 / 16, in1=v_side[:, 3:132],
-            op0=ALU.mult, op1=ALU.mult, accum_out=v_neg[:],
-        )
-        centre_xs()
-        y2_sum = small("y2_sum", G)
-        vec.tensor_reduce(out=y2_sum[:, 0 : G // 2], in_=runs(y2[:, left]), axis=AXIS.X, op=ALU.add)
+        centre(w_side[:, 0:128], xs[:, 4:132], "x_blocks")()
         h_f = sb.tile([P, 2, G], F32, name="h_f")
         vec.scalar_tensor_tensor(
             out=h_f[:], in0=slopes[:, 1:4:2, :], scalar=z_16th, in1=times(w_side[:, 0:64], 2),
             op0=ALU.mult, op1=ALU.mult,
+        )
+        coefs = sb.tile([P, 2, G], F32, name="coefs")
+        vec.scalar_tensor_tensor(
+            out=coefs[:], in0=times(w_side[:, 64:128], 2), scalar=z_16th, in1=h_f[:], op0=ALU.mult, op1=ALU.add
+        )
+        centre_pis()
+        for h, cols in enumerate((left, right)):
+            vec.scalar_tensor_tensor(
+                out=spare[:, cols], in0=p[:, cols], scalar=z_inv[:], in1=y[:, cols], op0=ALU.mult, op1=ALU.mult,
+                accum_out=v_side[:, 2 + h : 3 + h],
+            )
+        v_neg = small("v_neg", 1)
+        spare_v = small("spare_v", 130)
+        vec.scalar_tensor_tensor(
+            out=spare_v[:], in0=xs[:, 2:132], scalar=-1.0 / 16, in1=v_side[:, 2:132],
+            op0=ALU.mult, op1=ALU.mult, accum_out=v_neg[:],
         )
         w_neg = small("w_neg", 1)
         spare_w = small("spare_w", 129)
@@ -235,61 +234,60 @@ def tile_attend_gpblockcontrast_kernel(tc, query, keys_words, keys_scales, steep
         )
         w_neg_p = small("w_neg_p", 1)
         act.activation(out=w_neg_p[:], in_=w_neg[:], func=ACT.Copy, scale=two_k)
-        coefs = sb.tile([P, 2, G], F32, name="coefs")
-        vec.scalar_tensor_tensor(
-            out=coefs[:], in0=times(w_side[:, 64:128], 2), scalar=z_16th, in1=h_f[:], op0=ALU.mult, op1=ALU.add
-        )
-        vec.tensor_reduce(out=y2_sum[:, G // 2 : G], in_=runs(y2[:, right]), axis=AXIS.X, op=ALU.add)
         moved = wide("moved")
-        vec.scalar_tensor_tensor(
-            out=runs(moved[:]), in0=spread(coefs[:, 0, :]), scalar=v_neg[:], in1=runs(y[:]), op0=ALU.add, op1=ALU.add
-        )
         move2 = small("move2", G)
-        act.activation(out=move2[:], in_=coefs[:, 0, :], func=ACT.Square, bias=v_neg[:])
         square = wide("square")
-        for cols in (left, right):
-            act.activation(out=square[:, cols], in_=moved[:, cols], func=ACT.Square, scale=root_k)
+        terms = sb.tile([P, 2, G], F32, name="terms")
+        y2_sum = small("y2_sum", G)
         n0 = small("n0", G)
+        m_part = small("m_part", G)
+        m_blocks = small("m_blocks", BLOCKS)
+        m_sum = small("m_sum", G)
+        shift = small("shift", G)
+        t2 = wide("t2")
+        t3 = wide("t3")
+        result = wide("result")
+        act.activation(out=move2[:], in_=coefs[:, 0, :], func=ACT.Square, bias=v_neg[:])
+        for cols in (left, right):
+            vec.tensor_reduce(
+                out=y2_sum[:, cols.start // RUN : cols.stop // RUN], in_=runs(y2[:, cols]), axis=AXIS.X, op=ALU.add
+            )
         vec.scalar_tensor_tensor(
             out=n0[:], in0=y2_sum[:], scalar=z_half, in1=slopes[:, 1, :], op0=ALU.mult, op1=ALU.mult
         )
-        terms = sb.tile([P, 2, G], F32, name="terms")
-        vec.scalar_tensor_tensor(
-            out=terms[:, 0, :], in0=coefs[:, 1, :], scalar=v_neg[:], in1=x_f, op0=ALU.add, op1=ALU.mult
-        )
-        m_part = small("m_part", G)
         vec.scalar_tensor_tensor(
             out=terms[:, 1, :], in0=pis[:, 0, :], scalar=w_neg[:], in1=n0[:], op0=ALU.mult, op1=ALU.add
         )
         vec.scalar_tensor_tensor(
-            out=m_part[:], in0=move2[:], scalar=neg_four, in1=terms[:, 0, :], op0=ALU.mult, op1=ALU.add
+            out=m_part[:], in0=move2[:], scalar=neg_four, in1=terms[:, 1, :], op0=ALU.mult, op1=ALU.add
         )
-        t2 = wide("t2")
-
-        def add_p(cols):
-            vec.scalar_tensor_tensor(
-                out=t2[:, cols], in0=p[:, cols], scalar=w_neg_p[:], in1=base_sb[:, cols], op0=ALU.mult, op1=ALU.add
-            )
-
-        add_p(left)
-        m_blocks = small("m_blocks", BLOCKS)
+        vec.scalar_tensor_tensor(
+            out=terms[:, 0, :], in0=coefs[:, 1, :], scalar=v_neg[:], in1=x_f, op0=ALU.add, op1=ALU.mult
+        )
         vec.tensor_reduce(
             out=m_blocks[:], in_=terms[:].rearrange("p t (b j) -> p b t j", j=RUN), axis=AXIS.XY, op=ALU.add
         )
-        m_sum = small("m_sum", G)
-        vec.tensor_tensor(out=m_sum[:], in0=m_part[:], in1=terms[:, 1, :], op=ALU.add)
-        add_p(right)
-        shift = small("shift", G)
+        vec.tensor_tensor(out=m_sum[:], in0=m_part[:], in1=terms[:, 0, :], op=ALU.add)
         vec.scalar_tensor_tensor(
             out=runs(shift[:]), in0=spread(m_blocks[:]), scalar=-1.0 / RUN, in1=runs(m_sum[:]), op0=ALU.mult, op1=ALU.add
         )
-        t3 = wide("t3")
-        result = wide("result")
-        for h, cols in enumerate((left, right)):
+        for cols in (left, right):
             vec.scalar_tensor_tensor(
-                out=runs(t3[:, cols]), in0=spread(shift[:, h * G // 2 : (h + 1) * G // 2]), scalar=quarter_k,
-                in1=runs(t2[:, cols]), op0=ALU.mult, op1=ALU.add,
+                out=runs(moved[:, cols]), in0=spread(coefs[:, 0, cols.start // RUN : cols.stop // RUN]), scalar=v_neg[:],
+                in1=runs(y[:, cols]), op0=ALU.add, op1=ALU.add,
+            )
+            act.activation(out=square[:, cols], in_=moved[:, cols], func=ACT.Square, scale=z_inv[:])
+        for cols in (left, right):
+            vec.scalar_tensor_tensor(
+                out=t2[:, cols], in0=p[:, cols], scalar=w_neg_p[:], in1=base_sb[:, cols], op0=ALU.mult, op1=ALU.add
+            )
+        for cols in (left, right):
+            vec.scalar_tensor_tensor(
+                out=t3[:, cols], in0=square[:, cols], scalar=PENALTY, in1=t2[:, cols], op0=ALU.mult, op1=ALU.add
             )
         for cols, queue in ((left, nc.sync), (right, nc.scalar)):
-            vec.tensor_tensor(out=result[:, cols], in0=t3[:, cols], in1=square[:, cols], op=ALU.add)
+            vec.scalar_tensor_tensor(
+                out=runs(result[:, cols]), in0=spread(shift[:, cols.start // RUN : cols.stop // RUN]), scalar=quarter_k,
+                in1=runs(t3[:, cols]), op0=ALU.mult, op1=ALU.add,
+            )
             queue.dma_start(out[:, cols], result[:, cols])

@@ -75,26 +75,28 @@ def tile_attend_gpblockcontrast_kernel(tc, query, keys_words, keys_scales, steep
         vec.memset(k_bytes[:].bitcast(I32), 0)
         nc.gpsimd.memset(v_bytes[:].bitcast(I32), 0)
         nc.sync.dma_start(offsets[:], offs)
-        nc.sync.dma_start(s_col[:], steep)
+        nc.sync.dma_start(k_words[:].bitcast(I32), keys_words[0].bitcast(I32))
         for quad in range(4):
             nc.sync.dma_start(
                 k_bytes[32 * quad : 32 * quad + 4, :].bitcast(I32), keys_scales[0, 4 * quad : 4 * quad + 4, :].bitcast(I32)
             )
-        nc.sync.dma_start(k_words[:].bitcast(I32), keys_words[0].bitcast(I32))
-        nc.sync.dma_start(q_raw[:], query.rearrange("(p j) w -> p j w", j=PACK))
         nc.sync.dma_start(g_raw[:], gout.rearrange("(p j) w -> p j w", j=PACK))
-        nc.sync.dma_start(v_words[:].bitcast(I32), vals_words[0].bitcast(I32))
+        nc.sync.dma_start(q_raw[:], query.rearrange("(p j) w -> p j w", j=PACK))
         for quad in range(4):
             nc.sync.dma_start(
                 v_bytes[32 * quad : 32 * quad + 4, :].bitcast(I32), vals_scales[0, 4 * quad : 4 * quad + 4, :].bitcast(I32)
             )
+        nc.sync.dma_start(v_words[:].bitcast(I32), vals_words[0].bitcast(I32))
+        nc.gpsimd.dma_start(s_col[:], steep)
 
         factors = small("factors", 9)
         for col, value in enumerate((1.0 / 16, 0.5, -0.5, -1.0, 1.0 / 16, 0.5, 2 * PENALTY, PENALTY / 4, -4.0)):
             vec.memset(factors[:, col : col + 1], value)
 
         s_mult = small("s_mult", 4)
-        vec.tensor_scalar(out=s_mult[:], in0=factors[:, 0:4], scalar1=s_col[:], scalar2=None, op0=ALU.mult)
+        nc.gpsimd.tensor_scalar(
+            out=s_mult[:], in0=factors[:, 0:4], scalar1=s_col[:], scalar2=0.0, op0=ALU.mult, op1=ALU.add
+        )
         s_16th, s_half, s_neg_half, s_neg = (s_mult[:, col : col + 1] for col in range(4))
         slopes = sb.tile([P, 4, G], F32, name="slopes")
         vec.memset(slopes[:, 2, :], 1.0)
@@ -102,9 +104,9 @@ def tile_attend_gpblockcontrast_kernel(tc, query, keys_words, keys_scales, steep
         vec.memset(xs[:, 2:4], 8.0)
         vec.memset(xs[:, 196:197], 8.0)
 
-        def quantise(raw, name):
+        def quantise(raw, name, codes_tag):
             woven = sb.tile([P, P, PACK], BF16, name=name + "_woven", tag=name + "_woven", align_bytes=64)
-            codes = sb.tile([P, P], U32, name=name + "_codes", align_bytes=64)
+            codes = sb.tile([P, P], U32, name=name + "_codes", tag=codes_tag, align_bytes=64)
             scales = sb.tile([P, P], U8, name=name + "_scales", align_bytes=64)
             act.activation(out=woven[:], in_=raw[:].rearrange("p j w -> p w j"), func=ACT.Copy)
             return codes, scales, lambda: vec.quantize_mx(
@@ -116,8 +118,8 @@ def tile_attend_gpblockcontrast_kernel(tc, query, keys_words, keys_scales, steep
             vec.tensor_copy(out=got[:], in_=window[:].indirect(offsets[:, first // 16 : (first + count) // 16]))
             return got
 
-        q_codes, q_scales, q_quant = quantise(q_raw, "q")
-        g_codes, g_scales, g_quant = quantise(g_raw, "g")
+        q_codes, q_scales, q_quant = quantise(q_raw, "q", "q_codes")
+        g_codes, g_scales, g_quant = quantise(g_raw, "g", "q_woven")
         base_sb = sb.tile([P, SLOTS], F32, name="base_sb", tag="q_then_base")
         nc.sync.dma_start(base_sb[:], base)
 
@@ -129,19 +131,19 @@ def tile_attend_gpblockcontrast_kernel(tc, query, keys_words, keys_scales, steep
             out=a_ps[:], lhsT=q_codes[:].bitcast(FP8X4), lhsT_scale=q_scales[:],
             rhs=kw[:].bitcast(FP4X4), rhs_scale=kb[:], start=True, stop=True,
         )
-        vw = gather(v_words, U16, "vw", tag="q_woven")
+        vb = gather(v_bytes, U8, "vb")
         g_quant()
         c_ps = ps.tile([P, SLOTS], F32, name="c_ps")
 
         def values_half(h, tag):
             cols = slice(h * SLOTS // 2, (h + 1) * SLOTS // 2)
-            vb = gather(v_bytes, U8, "vb%d" % h, tag=tag, first=cols.start, count=SLOTS // 2)
+            vw = gather(v_words, U16, "vw%d" % h, tag=tag, first=cols.start, count=SLOTS // 2)
             nc.tensor.matmul_mx(
                 out=c_ps[:, cols], lhsT=g_codes[:].bitcast(FP8X4), lhsT_scale=g_scales[:],
-                rhs=vw[:, cols].bitcast(FP4X4), rhs_scale=vb[:], start=True, stop=True,
+                rhs=vw[:].bitcast(FP4X4), rhs_scale=vb[:, cols], start=True, stop=True,
             )
 
-        values_half(0, "kb")
+        values_half(0, None)
 
         root = wide("root")
         root_sum = small("root_sum", 1, tag="root_sum")

@@ -76,18 +76,14 @@ def tile_attend_gpblockcontrast_kernel(tc, query, keys_words, keys_scales, steep
         nc.gpsimd.memset(v_bytes[:].bitcast(I32), 0)
         nc.sync.dma_start(offsets[:], offs)
         nc.sync.dma_start(k_words[:].bitcast(I32), keys_words[0].bitcast(I32))
-        for quad in range(4):
-            nc.sync.dma_start(
-                k_bytes[32 * quad : 32 * quad + 4, :].bitcast(I32), keys_scales[0, 4 * quad : 4 * quad + 4, :].bitcast(I32)
-            )
+        for r in range(4):
+            nc.sync.dma_start(k_bytes[r:P:32, :].bitcast(I32), keys_scales[0, r:16:4, :].bitcast(I32))
         nc.sync.dma_start(g_raw[:], gout.rearrange("(p j) w -> p j w", j=PACK))
         nc.sync.dma_start(q_raw[:], query.rearrange("(p j) w -> p j w", j=PACK))
-        for quad in range(4):
-            nc.sync.dma_start(
-                v_bytes[32 * quad : 32 * quad + 4, :].bitcast(I32), vals_scales[0, 4 * quad : 4 * quad + 4, :].bitcast(I32)
-            )
+        for r in range(4):
+            nc.sync.dma_start(v_bytes[r:P:32, :].bitcast(I32), vals_scales[0, r:16:4, :].bitcast(I32))
         nc.sync.dma_start(v_words[:].bitcast(I32), vals_words[0].bitcast(I32))
-        nc.gpsimd.dma_start(s_col[:], steep)
+        nc.sync.dma_start(s_col[:], steep)
 
         factors = small("factors", 9)
         for col, value in enumerate((1.0 / 16, 0.5, -0.5, -1.0, 1.0 / 16, 0.5, 2 * PENALTY, PENALTY / 4, -4.0)):
@@ -108,7 +104,10 @@ def tile_attend_gpblockcontrast_kernel(tc, query, keys_words, keys_scales, steep
             woven = sb.tile([P, P, PACK], BF16, name=name + "_woven", tag=name + "_woven", align_bytes=64)
             codes = sb.tile([P, P], U32, name=name + "_codes", tag=codes_tag, align_bytes=64)
             scales = sb.tile([P, P], U8, name=name + "_scales", align_bytes=64)
-            act.activation(out=woven[:], in_=raw[:].rearrange("p j w -> p w j"), func=ACT.Copy)
+            act.activation(
+                out=woven[:].rearrange("p (c i) j -> p c j i", i=PACK),
+                in_=raw[:].rearrange("p j (c i) -> p c j i", i=PACK), func=ACT.Copy,
+            )
             return codes, scales, lambda: vec.quantize_mx(
                 out=codes[:].bitcast(FP8X4), scales=scales[:], in_=woven[:].rearrange("p w j -> p (w j)")
             )

from contextlib import ExitStack

import concourse.mybir as mybir

F32 = mybir.dt.float32
BF16 = mybir.dt.bfloat16
I32 = mybir.dt.int32
U32 = mybir.dt.uint32
U16 = mybir.dt.uint16
U8 = mybir.dt.uint8
FP8X4 = mybir.dt.float8_e4m3fn_x4
FP4X4 = mybir.dt.float4_e2m1fn_x4
ACT = mybir.ActivationFunctionType
ALU = mybir.AluOpType
AXIS = mybir.AxisListType

P = 128
PACK = 4
POOL = 2048
SLOTS = 512
RUN = 8
GROUPS = SLOTS // RUN
BLOCKS = GROUPS // RUN
PENALTY = 512.0 * 2.0 * 512.0

FLOPS = 2 * 2 * 512 * P * SLOTS


def runs(ap):
    return ap.rearrange("p (n j) -> p n j", j=RUN)


def spread(ap):
    return ap.unsqueeze(2).to_broadcast([P, ap.shape[1], RUN])


def times(ap, n):
    return ap.unsqueeze(1).to_broadcast([P, n, ap.shape[1]])


def tile_attend_gpblockcontrast_kernel(tc, query, keys_words, keys_scales, steep, gout, vals_words, vals_scales, base, offs, out):
    nc = tc.nc
    vec, act = nc.vector, nc.scalar
    G = GROUPS

    with ExitStack() as ctx:
        sb = ctx.enter_context(tc.tile_pool(name="sb", bufs=1))
        ps = ctx.enter_context(tc.psum_pool(name="ps", bufs=1))

        def wide(name):
            return sb.tile([P, SLOTS], F32, name=name)

        def small(name, width, tag=None):
            if tag is None:
                return sb.tile([P, width], F32, name=name)
            return sb.tile([P, width], F32, name=name, tag=tag, align_bytes=64)

        def centre(dst, src, name):
            n = src.shape[1] // RUN
            sums = small(name, n)
            vec.tensor_reduce(out=sums[:], in_=runs(src), axis=AXIS.X, op=ALU.add)
            return lambda: vec.scalar_tensor_tensor(
                out=runs(dst), in0=spread(sums[:]), scalar=-1.0 / RUN, in1=runs(src), op0=ALU.mult, op1=ALU.add
            )

        offsets = sb.tile([P, SLOTS // 16], U16, name="offsets")
        k_bytes = sb.tile([P, POOL], U8, name="k_bytes")
        v_bytes = sb.tile([P, POOL], U8, name="v_bytes")
        k_words = sb.tile([P, POOL], U16, name="k_words")
        v_words = sb.tile([P, POOL], U16, name="v_words")
        q_raw = sb.tile([P, PACK, P], F32, name="q_raw", tag="q_then_base")
        g_raw = sb.tile([P, PACK, P], F32, name="g_raw")
        s_col = small("s_col", 1)

        vec.memset(k_bytes[:].bitcast(I32), 0)
        nc.gpsimd.memset(v_bytes[:].bitcast(I32), 0)
        nc.sync.dma_start(offsets[:], offs)
        nc.sync.dma_start(k_words[:].bitcast(I32), keys_words[0].bitcast(I32))
        for r in range(4):
            nc.sync.dma_start(k_bytes[r:P:32, :].bitcast(I32), keys_scales[0, r:16:4, :].bitcast(I32))
        nc.sync.dma_start(g_raw[:], gout.rearrange("(p j) w -> p j w", j=PACK))
        nc.sync.dma_start(q_raw[:], query.rearrange("(p j) w -> p j w", j=PACK))
        for r in range(4):
            nc.sync.dma_start(v_bytes[r:P:32, :].bitcast(I32), vals_scales[0, r:16:4, :].bitcast(I32))
        nc.sync.dma_start(v_words[:].bitcast(I32), vals_words[0].bitcast(I32))
        nc.sync.dma_start(s_col[:], steep)

        factors = small("factors", 9)
        for col, value in enumerate((1.0 / 16, 0.5, -0.5, -1.0, 1.0 / 16, 0.5, 2 * PENALTY, PENALTY / 4, -4.0)):
            vec.memset(factors[:, col : col + 1], value)

        s_mult = small("s_mult", 4)
        nc.gpsimd.tensor_scalar(
            out=s_mult[:], in0=factors[:, 0:4], scalar1=s_col[:], scalar2=0.0, op0=ALU.mult, op1=ALU.add
        )
        s_16th, s_half, s_neg_half, s_neg = (s_mult[:, col : col + 1] for col in range(4))
        slopes = sb.tile([P, 4, G], F32, name="slopes")
        vec.memset(slopes[:, 2, :], 1.0)
        xs = small("xs", 200)
        vec.memset(xs[:, 2:4], 8.0)
        vec.memset(xs[:, 196:197], 8.0)

        def quantise(raw, name, codes_tag):
            woven = sb.tile([P, P, PACK], BF16, name=name + "_woven", tag=name + "_woven", align_bytes=64)
            codes = sb.tile([P, P], U32, name=name + "_codes", tag=codes_tag, align_bytes=64)
            scales = sb.tile([P, P], U8, name=name + "_scales", align_bytes=64)
            act.activation(
                out=woven[:].rearrange("p (c i) j -> p c j i", i=PACK),
                in_=raw[:].rearrange("p j (c i) -> p c j i", i=PACK), func=ACT.Copy,
            )
            return codes, scales, lambda: vec.quantize_mx(
                out=codes[:].bitcast(FP8X4), scales=scales[:], in_=woven[:].rearrange("p w j -> p (w j)")
            )

        def gather(window, dtype, name, tag=None, first=0, count=SLOTS):
            got = sb.tile([P, count], dtype, name=name, tag=tag or name, align_bytes=64)
            vec.tensor_copy(out=got[:], in_=window[:].indirect(offsets[:, first // 16 : (first + count) // 16]))
            return got

        q_codes, q_scales, q_quant = quantise(q_raw, "q", "q_codes")
        g_codes, g_scales, g_quant = quantise(g_raw, "g", "q_woven")
        base_sb = sb.tile([P, SLOTS], F32, name="base_sb", tag="q_then_base")
        nc.sync.dma_start(base_sb[:], base)

        kb = gather(k_bytes, U8, "kb")
        kw = gather(k_words, U16, "kw")
        q_quant()
        a_ps = ps.tile([P, SLOTS], F32, name="a_ps")
        nc.tensor.matmul_mx(
            out=a_ps[:], lhsT=q_codes[:].bitcast(FP8X4), lhsT_scale=q_scales[:],
            rhs=kw[:].bitcast(FP4X4), rhs_scale=kb[:], start=True, stop=True,
        )
        vb = gather(v_bytes, U8, "vb")
        g_quant()
        c_ps = ps.tile([P, SLOTS], F32, name="c_ps")

        def values_half(h, tag):
            cols = slice(h * SLOTS // 2, (h + 1) * SLOTS // 2)
            vw = gather(v_words, U16, "vw%d" % h, tag=tag, first=cols.start, count=SLOTS // 2)
            nc.tensor.matmul_mx(
                out=c_ps[:, cols], lhsT=g_codes[:].bitcast(FP8X4), lhsT_scale=g_scales[:],
                rhs=vw[:].bitcast(FP4X4), rhs_scale=vb[:, cols], start=True, stop=True,
            )

        values_half(0, None)

        root = wide("root")
        root_sum = small("root_sum", 1, tag="root_sum")
        act.activation(out=root[:], in_=a_ps[:], func=ACT.Exp, scale=0.25, accum_out=root_sum[:])
        root_inv = small("root_inv", 1)
        vec.reciprocal(out=root_inv[:], in_=root_sum[:])
        half = wide("half")
        act.activation(out=half[:], in_=root[:], func=ACT.Square, scale=root_inv[:])
        e = wide("e")
        act.activation(out=e[:], in_=half[:], func=ACT.Square)

        a_sum = small("a_sum", G, tag="a_sum")
        vec.tensor_reduce(out=a_sum[:], in_=runs(a_ps[:]), axis=AXIS.X, op=ALU.add)
        contrast = small("contrast", G)
        centre(contrast[:], a_sum[:], "a_blocks")()
        values_half(1, "a_sum")

        th = small("th", G)
        act.activation(out=th[:], in_=contrast[:], func=ACT.Tanh, scale=s_16th)
        act.activation(out=slopes[:, 1, :], in_=th[:], func=ACT.Identity, scale=s_neg_half, bias=s_half)
        act.activation(out=slopes[:, 3, :], in_=th[:], func=ACT.Copy, scale=s_neg)
        act.activation(out=slopes[:, 0, :], in_=slopes[:, 1, :], func=ACT.Copy, bias=1.0)

        left, right = slice(0, SLOTS // 2), slice(SLOTS // 2, SLOTS)
        p = wide("p")
        z = small("z", 1)
        vec.scalar_tensor_tensor(
            out=runs(p[:]), in0=spread(th[:]), scalar=1.0, in1=runs(e[:]), op0=ALU.add, op1=ALU.mult, accum_out=z[:]
        )
        mass = small("mass", G)
        vec.tensor_reduce(out=mass[:, 0 : G // 2], in_=runs(p[:, left]), axis=AXIS.X, op=ALU.add)
        z_inv = small("z_inv", 1)
        vec.reciprocal(out=z_inv[:], in_=z[:])
        vec.tensor_reduce(out=mass[:, G // 2 : G], in_=runs(p[:, right]), axis=AXIS.X, op=ALU.add)
        z_mult = small("z_mult", 5)
        act.activation(out=z_mult[:, 0:2], in_=factors[:, 4:6], func=ACT.Copy, scale=z[:])
        act.activation(out=z_mult[:, 2:5], in_=factors[:, 6:9], func=ACT.Copy, scale=z_inv[:])
        z_16th, z_half, two_k, quarter_k, neg_four = (z_mult[:, col : col + 1] for col in range(5))
        spare = wide("spare")
        c_mean = small("c_mean", 1)
        vec.scalar_tensor_tensor(
            out=spare[:], in0=c_ps[:], scalar=z_inv[:], in1=p[:], op0=ALU.mult, op1=ALU.mult, accum_out=c_mean[:]
        )
        pis = sb.tile([P, 2, G], F32, name="pis")
        vec.tensor_tensor(out=pis[:], in0=slopes[:, 1:3, :], in1=times(mass[:], 2), op=ALU.mult)
        y = wide("y")
        vec.scalar_tensor_tensor(
            out=y[:], in0=c_ps[:], scalar=c_mean[:], in1=p[:], op0=ALU.subtract, op1=ALU.mult
        )
        v_side = small("v_side", 132)
        centre_pis = centre(v_side[:, 4:132], pis[:].rearrange("p t g -> p (t g)"), "pi_blocks")
        w_side = small("w_side", 129)
        y2 = wide("y2")
        act.activation(out=y2[:], in_=y[:], func=ACT.Square, scale=z_inv[:], accum_out=w_side[:, 128:129])

        y_sum = small("y_sum", G)
        vec.tensor_reduce(out=y_sum[:], in_=runs(y[:]), axis=AXIS.X, op=ALU.add)
        vec.scalar_tensor_tensor(
            out=xs[:, 4:196].rearrange("p (t g) -> p t g", t=3), in0=slopes[:, 0:3, :], scalar=z_inv[:],
            in1=times(y_sum[:], 3), op0=ALU.mult, op1=ALU.mult,
        )
        x_f = xs[:, 68:132]
        centre(w_side[:, 0:128], xs[:, 4:132], "x_blocks")()
        h_f = sb.tile([P, 2, G], F32, name="h_f")
        vec.scalar_tensor_tensor(
            out=h_f[:], in0=slopes[:, 1:4:2, :], scalar=z_16th, in1=times(w_side[:, 0:64], 2),
            op0=ALU.mult, op1=ALU.mult,
        )
        coefs = sb.tile([P, 2, G], F32, name="coefs")
        vec.scalar_tensor_tensor(
            out=coefs[:], in0=times(w_side[:, 64:128], 2), scalar=z_16th, in1=h_f[:], op0=ALU.mult, op1=ALU.add
        )
        centre_pis()
        for h, cols in enumerate((left, right)):
            vec.scalar_tensor_tensor(
                out=spare[:, cols], in0=p[:, cols], scalar=z_inv[:], in1=y[:, cols], op0=ALU.mult, op1=ALU.mult,
                accum_out=v_side[:, 2 + h : 3 + h],
            )
        v_neg = small("v_neg", 1)
        spare_v = small("spare_v", 130)
        vec.scalar_tensor_tensor(
            out=spare_v[:], in0=xs[:, 2:132], scalar=-1.0 / 16, in1=v_side[:, 2:132],
            op0=ALU.mult, op1=ALU.mult, accum_out=v_neg[:],
        )
        w_neg = small("w_neg", 1)
        spare_w = small("spare_w", 129)
        vec.scalar_tensor_tensor(
            out=spare_w[:], in0=w_side[:], scalar=-1.0 / 16, in1=xs[:, 68:197],
            op0=ALU.mult, op1=ALU.mult, accum_out=w_neg[:],
        )
        w_neg_p = small("w_neg_p", 1)
        act.activation(out=w_neg_p[:], in_=w_neg[:], func=ACT.Copy, scale=two_k)
        moved = wide("moved")
        move2 = small("move2", G)
        square = wide("square")
        terms = sb.tile([P, 2, G], F32, name="terms")
        y2_sum = small("y2_sum", G)
        n0 = small("n0", G)
        m_part = small("m_part", G)
        m_blocks = small("m_blocks", BLOCKS)
        m_sum = small("m_sum", G)
        shift = small("shift", G)
        t2 = wide("t2")
        t3 = wide("t3")
        result = wide("result")
        act.activation(out=move2[:], in_=coefs[:, 0, :], func=ACT.Square, bias=v_neg[:])
        for cols in (left, right):
            vec.tensor_reduce(
                out=y2_sum[:, cols.start // RUN : cols.stop // RUN], in_=runs(y2[:, cols]), axis=AXIS.X, op=ALU.add
            )
        vec.scalar_tensor_tensor(
            out=n0[:], in0=y2_sum[:], scalar=z_half, in1=slopes[:, 1, :], op0=ALU.mult, op1=ALU.mult
        )
        vec.scalar_tensor_tensor(
            out=terms[:, 1, :], in0=pis[:, 0, :], scalar=w_neg[:], in1=n0[:], op0=ALU.mult, op1=ALU.add
        )
        vec.scalar_tensor_tensor(
            out=m_part[:], in0=move2[:], scalar=neg_four, in1=terms[:, 1, :], op0=ALU.mult, op1=ALU.add
        )
        vec.scalar_tensor_tensor(
            out=terms[:, 0, :], in0=coefs[:, 1, :], scalar=v_neg[:], in1=x_f, op0=ALU.add, op1=ALU.mult
        )
        vec.tensor_reduce(
            out=m_blocks[:], in_=terms[:].rearrange("p t (b j) -> p b t j", j=RUN), axis=AXIS.XY, op=ALU.add
        )
        vec.tensor_tensor(out=m_sum[:], in0=m_part[:], in1=terms[:, 0, :], op=ALU.add)
        vec.scalar_tensor_tensor(
            out=runs(shift[:]), in0=spread(m_blocks[:]), scalar=-1.0 / RUN, in1=runs(m_sum[:]), op0=ALU.mult, op1=ALU.add
        )
        for cols in (left, right):
            vec.scalar_tensor_tensor(
                out=runs(moved[:, cols]), in0=spread(coefs[:, 0, cols.start // RUN : cols.stop // RUN]), scalar=v_neg[:],
                in1=runs(y[:, cols]), op0=ALU.add, op1=ALU.add,
            )
            act.activation(out=square[:, cols], in_=moved[:, cols], func=ACT.Square, scale=z_inv[:])
        for cols in (left, right):
            vec.scalar_tensor_tensor(
                out=t2[:, cols], in0=p[:, cols], scalar=w_neg_p[:], in1=base_sb[:, cols], op0=ALU.mult, op1=ALU.add
            )
        for cols in (left, right):
            vec.scalar_tensor_tensor(
                out=t3[:, cols], in0=square[:, cols], scalar=PENALTY, in1=t2[:, cols], op0=ALU.mult, op1=ALU.add
            )
        for cols, queue in ((left, nc.sync), (right, nc.scalar)):
            vec.scalar_tensor_tensor(
                out=runs(result[:, cols]), in0=spread(shift[:, cols.start // RUN : cols.stop // RUN]), scalar=quarter_k,
                in1=runs(t3[:, cols]), op0=ALU.mult, op1=ALU.add,
            )
            queue.dma_start(out[:, cols], result[:, cols])
